import numpy as np, ml_dtypes
CORES = [10,34,74,98]
N = 4
import mx_ref
NC, G = 512, 4
C = np.float32(0.019)
CNT = [[112,112,48,240],[144,368,0,0],[0,32,208,272],[256,0,256,0]]
OFF = [[sum(c[:e]) for e in range(N + 1)] for c in CNT]
BF = ml_dtypes.bfloat16
def cut(t, i, w=512):
    return t[:, w * i:w * i + w]
def tile(rs):
    return np.stack(rs, axis=2).reshape(128, -1).astype(BF)
def layer(w, X):
    out = []
    for i in range(G):
        for t in range(len(X)):
            p = mx_ref.matmul(mx_ref.quantize(cut(w, len(X) * i + t)), X[t])
            z = p if t == 0 else z + p
        out.append(z)
    return out
def act(Z):
    return [np.maximum(z, 0) * C for z in Z]
def setup_inputs(rng):
    def f(*shape):
        return mx_ref.flush((rng.standard_normal(shape, dtype=np.float32) * np.exp2(rng.integers(-2, 3, shape[:-1] + (1,)))).astype(BF))
    return {"x": f(N, 128, 4 * NC), "w1": f(N, 128, G * 512), "w2": f(N, 128, 512), "s1": f(N, 128, G * 512), "s2": f(N, 128, 512)}
def setup_inputs_blocks(rng):
    d = setup_inputs(rng)
    for k in ("x", "w1", "w2", "s1", "s2"): d[k] = mx_ref.spread(d[k], rng, 4)
    return d
def setup_inputs_wide(rng):
    d = setup_inputs(rng)
    for k in ("x", "w1", "w2", "s1", "s2"): d[k] = mx_ref.flush((d[k].astype(np.float32) * np.exp2(rng.integers(-8, 9, (N, 1, 1))).astype(np.float32)).astype(BF))
    return d
def setup_inputs_zeros(rng):
    d = setup_inputs(rng); v = d["x"].reshape(N, 128, -1, 4).copy()
    v[np.broadcast_to((rng.random((N, 1, v.shape[2], 1)) < 0.33), v.shape)] = 0
    d["x"] = v.reshape(d["x"].shape)
    return d
def reference(x, w1, w2, s1, s2):
    y = np.zeros((N, 128, NC), np.float32)
    for j in range(N):
        y[j] = mx_ref.matmul(mx_ref.quantize(s2[j]), mx_ref.quantize(tile(act(layer(s1[j], [mx_ref.quantize(x[j])])))))
    for e in range(N):
        t = np.concatenate([x[j][:, 4 * OFF[j][e]:4 * OFF[j][e + 1]] for j in range(N)], axis=1)
        p = mx_ref.matmul(mx_ref.quantize(w2[e]), mx_ref.quantize(tile(act(layer(w1[e], [mx_ref.quantize(t)])))))
        c = 0
        for j in range(N):
            a, b = OFF[j][e], OFF[j][e + 1]
            y[j][:, a:b] = y[j][:, a:b] + p[:, c:c + b - a]; c += b - a
    return {"y": y}

from concourse.bass import DstId, RemoteDMATransfer
from concourse.mybir import dt, AluOpType, ActivationFunctionType as AF

C = 0.019
BF, F8, U8, F32 = "bfloat16", "float8_e4m3fn_x4", "uint8", "float32"
SCRATCH = {
    "xb": ("sbuf", [128, 2048], BF), "xq": ("sbuf", [128, 512], F8), "xs": ("sbuf", [128, 512], U8),
    "w1b": ("sbuf", [128, 2048], BF), "w1q": ("sbuf", [128, 512], F8), "w1s": ("sbuf", [128, 512], U8),
    "s1b": ("sbuf", [128, 2048], BF), "s1q": ("sbuf", [128, 512], F8), "s1s": ("sbuf", [128, 512], U8),
    "w2b": ("sbuf", [128, 512], BF), "w2q": ("sbuf", [128, 128], F8), "w2s": ("sbuf", [128, 128], U8),
    "s2b": ("sbuf", [128, 512], BF), "s2q": ("sbuf", [128, 128], F8), "s2s": ("sbuf", [128, 128], U8),
    "kb": ("sbuf", [128, 2048], BF), "kq": ("sbuf", [128, 512], F8), "ks": ("sbuf", [128, 512], U8),
    "hb": ("sbuf", [128, 2560], BF), "hq": ("sbuf", [128, 640], F8), "hs": ("sbuf", [128, 640], U8),
    "gb": ("sbuf", [128, 2048], BF), "gq": ("sbuf", [128, 512], F8), "gs": ("sbuf", [128, 512], U8),
    "lq": ("sbuf", [128, 640], F8), "ls": ("sbuf", [128, 640], U8),
    "pb": ("sbuf", [128, 640], F32),
    "yl": ("sbuf", [128, 512], F32),
    "yb": ("sbuf", [128, 512], F32),
}
for _b in range(8):
    SCRATCH["ps%d" % _b] = ("psum", [128, 512], F32)

SEMAPHORES = (["lxA", "lxB", "ls1a", "ls1b", "ls2", "lw1a", "lw1b", "lw2", "gate", "osend", "oret",
               "qxA", "qxB", "qs1a", "qs1b", "qs2", "qw1a", "qw1b", "qw2", "usem", "yhs", "st", "sth"]
              + ["xin%d" % j for j in range(4)] + ["pin%d" % e for e in range(4)]
              + ["add%d" % e for e in range(4)] + ["ev%d" % j for j in range(4)]
              + ["%s_%s%d" % (k, p, b) for k in ("S", "A", "B", "H") for p in ("m", "a") for b in range(4)]
              + ["%s_%s" % (k, p) for k in ("S", "A", "B", "H") for p in ("q", "p")])

PIECE = [((272, 512), (0, 272)), ((0, 144), (144, 512)), ((240, 512), (0, 240)), ((0, 256), (256, 512))]
SENDS = [
    [[("q", 3, 272, 240, "A")], [("s", 3, 272, 240, "A")],
     [("q", 1, 112, 128, "B"), ("q", 2, 224, 128, "B")], [("s", 1, 112, 128, "B"), ("s", 2, 224, 128, "B")]],
    [[("q", 0, 0, 144, "A")], [("s", 0, 0, 144, "A")]],
    [[("q", 3, 240, 272, "A")], [("s", 3, 240, 272, "A")], [("q", 1, 0, 32, "B"), ("s", 1, 0, 128, "B")]],
    [[("q", 0, 0, 256, "A"), ("q", 2, 256, 256, "B")], [("s", 0, 0, 256, "A"), ("s", 2, 256, 256, "B")]],
]
LAND = [{1: 0, 3: 144}, {0: 0, 2: 128}, {3: 0, 0: 256}, {2: 0, 0: 272}]
CHUNKS = [[(0, 144, [1]), (144, 256, [3])], [(0, 160, [0, 2])], [(0, 256, [3]), (256, 128, [0])], [(0, 272, [2]), (272, 240, [0])]]
HOME = [(0, 128), (144, 368), (32, 208), None]
OVERLAP = [False, False, False, True]
URANGE = [(112, 512), (0, 144), (0, 512), (0, 512)]
BACK = [[1, 2, 3], [0], [1, 3], [2, 0]]


def engines(topo, src, dst):
    m = topo.mask(src, dst)
    return [i for i in range(m.bit_length()) if m >> i & 1]


def rank_program(g, core, T, topo):
    r = T.rank_of(core)
    if r is None:
        return
    CNT = T.tables["CNT"]
    OFF = [[sum(c[:e]) for e in range(5)] for c in CNT]
    sem, te, ve, ac, sy = T.sem, g.tensor, g.vector, g.scalar, g.sync
    ps = [T["ps%d" % b] for b in range(8)]
    seen = {}

    def wait(q, name, val=1):
        key = (q[0], name)
        if seen.get(key, 0) < val:
            seen[key] = val
            q[1].wait_ge(sem[name], val)

    G, TE, VE, AC, SY = ("g", g), ("te", te), ("ve", ve), ("ac", ac), ("sy", sy)

    def load(q, name, dst, src, a, b):
        q[1].dma_start(dst[:, a:b], src[:, a:b]).then_inc(sem[name], 16)

    def quant(name, needs, q, s, src, a, n, qa):
        for nm, v in needs:
            wait(VE, nm, v)
        ve.quantize_mx(q[:, qa:qa + n], s[:, qa:qa + n], src[:, 4 * a:4 * (a + n)]).then_inc(sem[name], 1)

    def split(j, call):
        es = engines(topo, T.cores[j], T.cores[call[0][1]])
        w = len(es) // len(call)
        return [(t, sum(1 << i for i in es[k * w:(k + 1) * w]), w) for k, t in enumerate(call)]

    arrive = {}
    for j in range(4):
        for call in SENDS[j]:
            for t, m, w in split(j, call):
                arrive[(j, t[1])] = arrive.get((j, t[1]), 0) + w

    (A0, A1), (B0, B1) = PIECE[r]
    load(SY, "lxA", T.xb, T.x, 4 * A0, 4 * A1)
    load(AC, "lxB", T.xb, T.x, 4 * B0, 4 * B1)
    load(SY, "ls1a", T.s1b, T.s1, 0, 1024)
    load(AC, "ls1b", T.s1b, T.s1, 1024, 2048)
    load(AC, "ls2", T.s2b, T.s2, 0, 512)

    quant("qxA", [("lxA", 16)], T.xq, T.xs, T.xb, A0, A1 - A0, A0)
    quant("qxB", [("lxB", 16)], T.xq, T.xs, T.xb, B0, B1 - B0, B0)
    nsend = 0
    for k, call in enumerate(SENDS[r]):
        for t in call:
            wait(G, "qx" + t[4])
        trs = []
        for (kind, e, a, n, _), m, w in split(r, call):
            o = LAND[e][r]
            if kind == "q":
                src, dst = T.xq[:, a:a + n].bitcast(dt.uint8), T.lq[:, o:o + n].bitcast(dt.uint8)
            else:
                src, dst = T.xs[:, a:a + n], T.ls[:, o:o + n]
            rid, pid, _se = topo.addr(T.cores[e])
            trs.append((dst, src, sem["xin%d" % r], rid, pid, m))
            nsend += w
        if len(trs) == 1:
            dst, src, rs, rid, pid, m = trs[0]
            g.remote_dma(dst, src, rs, sem["osend"], pid, rid, m)
        else:
            g.remote_dma_fused([RemoteDMATransfer(dst_ids=[DstId(rid=rid, pnc=pid)], dma_engine_mask=m, remote_sem=rs,
                                                  src=src, dst=dst) for dst, src, rs, rid, pid, m in trs], local_sem=sem["osend"])
        if k == 1:
            g.sem_inc(sem["gate"], 1)

    wait(SY, "gate")
    load(SY, "lw1a", T.w1b, T.w1, 0, 1024)
    load(SY, "lw1b", T.w1b, T.w1, 1024, 2048)
    load(SY, "lw2", T.w2b, T.w2, 0, 512)

    def first(k, W, Ws, wneed, X, Xs, a, n, needs, bank, war):
        for b in range(4):
            for nm, v in needs + wneed(b):
                wait(TE, nm, v)
            if war:
                wait(TE, "%s_a%d" % (war, b))
            te.matmul_mx(ps[bank + b][:, 0:n], W[:, 128 * b:128 * b + 128], Ws[:, 128 * b:128 * b + 128],
                         X[:, a:a + n], Xs[:, a:a + n], True, True).then_inc(sem["%s_m%d" % (k, b)], 1)

    def acts(k, buf, a, n, bank, onv):
        for b in range(4):
            q = VE if b in onv else AC
            wait(q, "%s_m%d" % (k, b))
            out, z, s = buf[:, 4 * a + b:4 * (a + n):4], ps[bank + b][:, 0:n], sem["%s_a%d" % (k, b)]
            if b in onv:
                ve.tensor_scalar(out, z, 0.0, C, AluOpType.max, AluOpType.mult).then_inc(s, 1)
            else:
                ac.activation(out, z, AF.Relu, scale=C).then_inc(s, 1)

    def qtile(k, q, s, buf, a, n):
        quant(k + "_q", [("%s_a%d" % (k, b), 1) for b in range(4)], q, s, buf, a, n, a)

    sneed = lambda b: [("qs1a" if b < 2 else "qs1b", 1)]
    wneed = lambda b: [("qw1a" if b < 2 else "qw1b", 1)]

    quant("qs1a", [("ls1a", 16)], T.s1q, T.s1s, T.s1b, 0, 256, 0)
    quant("qs1b", [("ls1b", 16)], T.s1q, T.s1s, T.s1b, 256, 256, 256)
    quant("qs2", [("ls2", 16)], T.s2q, T.s2s, T.s2b, 0, 128, 0)
    first("S", T.s1q, T.s1s, sneed, T.xq, T.xs, 0, 512, [("qxA", 1), ("qxB", 1)], 0, None)
    acts("S", T.kb, 0, 512, 0, ())
    quant("qw1a", [("lw1a", 16)], T.w1q, T.w1s, T.w1b, 0, 256, 0)
    quant("qw1b", [("lw1b", 16)], T.w1q, T.w1s, T.w1b, 256, 256, 256)
    qtile("S", T.kq, T.ks, T.kb, 0, 512)
    quant("qw2", [("lw2", 16)], T.w2q, T.w2s, T.w2b, 0, 128, 0)

    u0, u1 = URANGE[r]
    chunks = CHUNKS[r]
    names = ["A", "B"][:len(chunks)]

    def one(i):
        a, n, js = chunks[i]
        first(names[i], T.w1q, T.w1s, wneed, T.lq, T.ls, a, n, [("xin%d" % j, arrive[(j, r)]) for j in js], 4,
              names[i - 1] if i else None)
        if i == 0:
            wait(TE, "qs2")
            wait(TE, "S_q")
            te.matmul_mx(ps[0][:, 0:u1 - u0], T.s2q[:, 0:128], T.s2s[:, 0:128], T.kq[:, u0:u1], T.ks[:, u0:u1],
                         True, True).then_inc(sem["usem"], 1)
        acts(names[i], T.hb, a, n, 4, (1, 3))
        qtile(names[i], T.hq, T.hs, T.hb, a, n)

    def two(i):
        a, n, js = chunks[i]
        k = names[i]
        wait(TE, "qw2")
        wait(TE, k + "_q")
        te.matmul_mx(ps[2 + i][:, 0:n], T.w2q[:, 0:128], T.w2s[:, 0:128], T.hq[:, a:a + n], T.hs[:, a:a + n],
                     True, True).then_inc(sem[k + "_p"], 1)
        for j in js:
            o, c = LAND[r][j], CNT[j][r]
            wait(AC, k + "_p")
            ac.activation(T.pb[:, o:o + c], ps[2 + i][:, o - a:o - a + c], AF.Copy).then_inc(sem["ev%d" % j], 1)
            wait(G, "ev%d" % j)
            rid, pid, _se = topo.addr(T.cores[j])
            g.remote_dma(T.yl[:, OFF[j][r]:OFF[j][r + 1]], T.pb[:, o:o + c], sem["pin%d" % r], sem["oret"], pid, rid,
                         topo.mask(core, T.cores[j]))

    one(0)
    if len(chunks) == 1:
        two(0)
    elif OVERLAP[r]:
        one(1)
        two(0)
        two(1)
    else:
        two(0)
        one(1)
        two(1)

    if HOME[r]:
        a, n = HOME[r]
        te.matmul_mx(ps[1][:, 0:n], T.s2q[:, 0:128], T.s2s[:, 0:128], T.kq[:, a:a + n], T.ks[:, a:a + n], True, False)
        first("H", T.w1q, T.w1s, wneed, T.xq, T.xs, a, n, [], 4, names[-1])
        acts("H", T.gb, 0, n, 4, (1, 3))
        qtile("H", T.gq, T.gs, T.gb, 0, n)
        wait(TE, "H_q")
        te.matmul_mx(ps[1][:, 0:n], T.w2q[:, 0:128], T.w2s[:, 0:128], T.gq[:, 0:n], T.gs[:, 0:n], False, True).then_inc(sem["H_p"], 1)
        c = CNT[r][r]
        wait(AC, "H_p")
        ac.activation(T.yb[:, a:a + c], ps[1][:, 0:c], AF.Copy).then_inc(sem["yhs"], 1)
        wait(AC, "yhs")
        ac.dma_start(T.y[:, a:a + c], T.yb[:, a:a + c]).then_inc(sem["sth"], 16)

    nst = 0
    wait(VE, "usem")
    for e in BACK[r]:
        a, b = OFF[r][e], OFF[r][e + 1]
        wait(VE, "pin%d" % e, len(engines(topo, T.cores[e], core)))
        ve.tensor_tensor(T.yb[:, a:b], ps[0][:, a - u0:b - u0], T.yl[:, a:b], AluOpType.add).then_inc(sem["add%d" % e], 1)
        wait(SY, "add%d" % e)
        sy.dma_start(T.y[:, a:b], T.yb[:, a:b]).then_inc(sem["st"], 16)
        nst += 16
    wait(SY, "st", nst)
    if HOME[r]:
        wait(AC, "sth", 16)
    wait(G, "osend", nsend)
    wait(G, "oret", sum(len(engines(topo, core, T.cores[j])) for _, _, js in chunks for j in js))
